import numpy as np
CORES = [4,20,36,52,68,84,100,116,132,148,164,180,196,212,228,244]
N = 16
TK = 128
NT = N * TK
EPS = 0.01
def setup_inputs(rng):
    x = (rng.standard_normal((N, 128, TK), dtype=np.float32) * (0.5 + np.arange(N, dtype=np.float32).reshape(N, 1, 1) / N) + rng.standard_normal((N, 128, 1), dtype=np.float32))
    return {"x": x, "dy": (rng.standard_normal((N, 128, TK), dtype=np.float32) + 0.5 * x + rng.standard_normal((1, 128, 1), dtype=np.float32))}
def setup_inputs_big(rng):
    d = setup_inputs(rng)
    for k in ("x", "dy"): d[k] = (d[k].astype(np.float32) * 1024.0).astype(d[k].dtype)
    return d
def setup_inputs_small(rng):
    d = setup_inputs(rng)
    for k in ("x", "dy"): d[k] = (d[k].astype(np.float32) * (1 / 1024.0)).astype(d[k].dtype)
    return d
def setup_inputs_apart(rng):
    d = setup_inputs(rng)
    f = (10.0 ** rng.permutation(np.linspace(-1.5, 1.5, N))).astype(np.float32).reshape(N, 1, 1)
    for k in ("x", "dy"): d[k] = (d[k].astype(np.float32) * f).astype(d[k].dtype)
    return d
def setup_inputs_mixed(rng):
    d = setup_inputs(rng)
    f = (10.0 ** rng.uniform(-3, 3, (1, 128, 1))).astype(np.float32); shape = rng.integers(3, size=(1, 128, 1))
    for k in ("x", "dy"):
        x = d[k].astype(np.float32)
        m = x.mean(axis=(0, 2), keepdims=True); level = m + np.sign(x - m) * np.abs(x - m).mean(axis=(0, 2), keepdims=True) * rng.uniform(0.9, 1.1, x.shape).astype(np.float32)
        other = x * np.where(rng.random(x.shape) < 0.5, 0.1, 1.0).astype(np.float32)
        d[k] = (np.where(shape == 1, level, np.where(shape == 2, other, x)) * f).astype(d[k].dtype)
    return d
def setup_inputs_offset(rng):
    d = setup_inputs(rng)
    x = d["x"]; spread = x.std(axis=(0, 2), keepdims=True)
    d["x"] = (x + spread * rng.uniform(16, 48, (1, 128, 1)) * rng.choice([-1.0, 1.0], (1, 128, 1))).astype(np.float32)
    return d
def reference(x, dy):
    X = x.astype(np.float64)
    mu = X.sum(axis=(0, 2)).reshape(1, 128, 1) / NT
    rs = 1.0 / np.sqrt(((X - mu) ** 2).sum(axis=(0, 2)).reshape(1, 128, 1) / NT + EPS)
    n = (X - mu) * rs
    DY = dy.astype(np.float64)
    a = DY.sum(axis=(0, 2)).reshape(1, 128, 1) / NT; c = (DY * n).sum(axis=(0, 2)).reshape(1, 128, 1) / NT
    return {"dx": (rs * (DY - a - n * c)).astype(np.float32)}

@@ -1,0 +1,145 @@
+from concourse.bass import DstId, RemoteDMATransfer
+from concourse.mybir import AluOpType, AxisListType, ActivationFunctionType
+
+N = 16
+TK = 128
+NT = N * TK
+EPS = 0.01
+
+SCRATCH = {
+    "xs": ("sbuf", [128, TK], "float32"),
+    "dys": ("sbuf", [128, TK], "float32"),
+    "st": ("sbuf", [128, 4], "float32"),
+    "gath": ("dram", [N, 128, 4], "float32"),
+    "G": ("sbuf", [N, 512], "float32"),
+    "Wc": ("sbuf", [N, 36], "float32"),
+    "ja": ("sbuf", [128, TK], "float32"),
+    "jb": ("sbuf", [128, TK], "float32"),
+    "jc": ("sbuf", [128, N], "float32"),
+    "pr": ("sbuf", [128, TK], "float32"),
+    "bn": ("sbuf", [128, N + 1], "float32"),
+    "ee": ("sbuf", [128, N], "float32"),
+    "sc": ("sbuf", [128, 8], "float32"),
+    "dya": ("sbuf", [128, TK], "float32"),
+    "uu": ("sbuf", [128, TK], "float32"),
+    "oo": ("sbuf", [128, TK], "float32"),
+    "yP": ("psum", [128, 512], "float32"),
+    "tP": ("psum", [128, 512], "float32"),
+    "P1": ("psum", [128, 512], "float32"),
+    "P2": ("psum", [128, 512], "float32"),
+    "P3": ("psum", [128, 512], "float32"),
+    "P4": ("psum", [128, 512], "float32"),
+}
+SEMAPHORES = ["ldx", "ldy", "cst", "cst2", "s_sx", "s_y", "s_pr", "s_st", "stq", "sent", "arr", "gl",
+              "m1", "m2", "m3", "m4", "q", "v", "iv", "rs", "bn", "e", "es", "w", "t", "dya", "u", "o", "std"]
+
+ADD, SUB, MUL = AluOpType.add, AluOpType.subtract, AluOpType.mult
+X = AxisListType.X
+ACT = ActivationFunctionType
+
+
+def rank_program(g, core, T, topo):
+    rank = T.rank_of(core)
+    if rank is None:
+        return
+    S = T.sem
+    V, A, PE, SY = g.vector, g.scalar, g.tensor, g.sync
+
+    SY.dma_start(T.xs[:], T.x[:]).then_inc(S.ldx, 16)
+    A.dma_start(T.dys[:], T.dy[:]).then_inc(S.ldy, 16)
+
+    V.memset(T.Wc[:, 0:16], 1.0 / NT).then_inc(S.cst, 1)
+    V.memset(T.Wc[:, 16:17], -1.0 / NT).then_inc(S.cst, 1)
+    V.memset(T.Wc[:, 17:33], 0.0).then_inc(S.cst, 1)
+    V.memset(T.Wc[:, 33:34], 1.0 / NT).then_inc(S.cst, 1)
+    V.memset(T.Wc[:, 34:35], 1.0 / (NT * TK * TK)).then_inc(S.cst, 1)
+    V.memset(T.Wc[:, 35:36], 1.0 / (NT * TK)).then_inc(S.cst, 1)
+    g.wait_ge(S.cst, 6)
+    g.affine_select(T.Wc[:, 0:16], T.Wc[:, 0:16], [[-1, N]], AluOpType.not_equal, 1.0 / NT - 1.0 / TK, 0, 1).then_inc(S.cst2, 1)
+    g.affine_select(T.Wc[:, 17:33], T.Wc[:, 17:33], [[-1, N]], AluOpType.not_equal, 1.0 / NT, 0, 1).then_inc(S.cst2, 1)
+
+    V.wait_ge(S.ldx, 16)
+    V.tensor_reduce(T.st[:, 0:1], T.xs[:], X, ADD, negate=True).then_inc(S.s_sx, 1)
+    V.wait_ge(S.s_sx, 1)
+    V.tensor_scalar(T.yP[:, 0:TK], T.xs[:], float(TK), T.st[:, 0:1], MUL, ADD).then_inc(S.s_y, 1)
+    V.wait_ge(S.s_y, 1)
+    V.wait_ge(S.ldy, 16)
+    V.tensor_tensor(T.pr[:], T.yP[:, 0:TK], T.dys[:], MUL).then_inc(S.s_pr, 1)
+    V.wait_ge(S.s_pr, 1)
+    V.tensor_reduce(T.st[:, 3:4], T.pr[:], X, ADD).then_inc(S.s_st, 1)
+
+    A.wait_ge(S.ldy, 16)
+    A.activation(T.ja[:], T.dys[:], ACT.Copy, accum_out=T.st[:, 2:3]).then_inc(S.s_st, 1)
+    A.wait_ge(S.ldx, 16)
+    A.wait_ge(S.s_sx, 1)
+    A.activation(T.jb[:], T.xs[:], ACT.Square, bias=T.st[:, 0:1], scale=float(TK), accum_out=T.st[:, 1:2]).then_inc(S.s_st, 1)
+
+    SY.wait_ge(S.s_sx, 1)
+    SY.wait_ge(S.s_st, 3)
+    SY.dma_start(T.gath[rank], T.st[:]).then_inc(S.stq, 16)
+
+    others = [T.cores[(rank + k) % N] for k in range(1, N)]
+    allowed = topo.mask(core, others[0])
+    for d in others:
+        allowed &= topo.mask(core, d)
+    engines = [e for e in range(16) if (allowed >> e) & 1]
+    engines = engines[::max(1, len(engines) // 4)][:4]
+    transfers = []
+    for j, e in enumerate(engines):
+        mine = others[j::len(engines)]
+        ids = []
+        for d in mine:
+            rid, pid = topo.addr(d, core)
+            ids.append(DstId(rid=rid, pnc=pid))
+        transfers.append(RemoteDMATransfer(dst_ids=ids, dma_engine_mask=1 << e, remote_sem=S.arr,
+                                           srcs=[T.gath[rank]], dsts=[T.gath[rank] for _ in mine], alu_op=0))
+    g.wait_ge(S.stq, 16)
+    g.remote_dma_fused(transfers, local_sem=S.sent)
+
+    SY.wait_ge(S.stq, 16)
+    SY.wait_ge(S.arr, N - 1)
+    SY.dma_start(T.G[:], T.gath[:]).then_inc(S.gl, 16)
+
+    PE.wait_ge(S.cst, 6)
+    PE.wait_ge(S.cst2, 2)
+    PE.wait_ge(S.gl, 16)
+    PE.matmul(T.P1[:, 0:17], T.G[:, 0:512:4], T.Wc[:, 0:17], True, True).then_inc(S.m1, 1)
+    PE.matmul(T.P2[:, 0:1], T.G[:, 1:512:4], T.Wc[:, 34:35], True, True).then_inc(S.m2, 1)
+    PE.matmul(T.P3[:, 0:17], T.G[:, 2:512:4], T.Wc[:, 17:34], True, True).then_inc(S.m3, 1)
+    PE.matmul(T.P4[:, 0:1], T.G[:, 3:512:4], T.Wc[:, 35:36], True, True).then_inc(S.m4, 1)
+
+    q, vv, iv, rs, es, w = (T.sc[:, k:k + 1] for k in range(6))
+    A.wait_ge(S.m1, 1)
+    A.activation(T.jc[:], T.P1[:, 0:N], ACT.Square, scale=0.25, accum_out=q).then_inc(S.q, 1)
+    V.wait_ge(S.q, 1)
+    V.wait_ge(S.m2, 1)
+    V.tensor_scalar(vv, q, T.P2[:, 0:1], EPS, ADD, ADD).then_inc(S.v, 1)
+    V.wait_ge(S.v, 1)
+    V.reciprocal(iv, vv).then_inc(S.iv, 1)
+    A.wait_ge(S.iv, 1)
+    A.activation(rs, iv, ACT.Sqrt).then_inc(S.rs, 1)
+
+    V.wait_ge(S.m3, 1)
+    V.tensor_copy(T.bn[:], T.P3[:, 0:17]).then_inc(S.bn, 1)
+    V.wait_ge(S.bn, 1)
+    V.tensor_scalar(T.dya[:], T.dys[:], T.bn[:, 16:17], None, SUB).then_inc(S.dya, 1)
+    V.tensor_tensor(T.ee[:], T.P1[:, 0:N], T.bn[:, 0:N], MUL).then_inc(S.e, 1)
+    V.wait_ge(S.e, 1)
+    V.tensor_reduce(es, T.ee[:], X, ADD).then_inc(S.es, 1)
+    V.wait_ge(S.es, 1)
+    V.wait_ge(S.m4, 1)
+    V.wait_ge(S.iv, 1)
+    V.tensor_scalar(w, es, T.P4[:, 0:1], iv, ADD, MUL).then_inc(S.w, 1)
+    V.wait_ge(S.w, 1)
+    V.tensor_scalar(T.tP[:, 0:TK], T.xs[:], T.P1[:, 16:17], w, SUB, MUL).then_inc(S.t, 1)
+    V.wait_ge(S.t, 1)
+    V.wait_ge(S.dya, 1)
+    V.tensor_tensor(T.uu[:], T.dya[:], T.tP[:, 0:TK], SUB).then_inc(S.u, 1)
+
+    A.wait_ge(S.rs, 1)
+    A.wait_ge(S.u, 1)
+    A.activation(T.oo[:], T.uu[:], ACT.Copy, scale=rs).then_inc(S.o, 1)
+    A.wait_ge(S.o, 1)
+    A.dma_start(T.dx[:], T.oo[:]).then_inc(S.std, 16)
+    A.wait_ge(S.std, 16)
+    g.wait_ge(S.sent, len(engines))

@@ -17,7 +17,7 @@ SCRATCH = {
     "jb": ("sbuf", [128, TK], "float32"),
     "jc": ("sbuf", [128, N], "float32"),
     "pr": ("sbuf", [128, TK], "float32"),
-    "bn": ("sbuf", [128, N + 1], "float32"),
+    "dS": ("sbuf", [128, N + 1], "float32"),
     "ee": ("sbuf", [128, N], "float32"),
     "sc": ("sbuf", [128, 8], "float32"),
     "dya": ("sbuf", [128, TK], "float32"),
@@ -31,7 +31,7 @@ SCRATCH = {
     "P4": ("psum", [128, 512], "float32"),
 }
 SEMAPHORES = ["ldx", "ldy", "cst", "cst2", "s_sx", "s_y", "s_pr", "s_st", "stq", "sent", "arr", "gl",
-              "m1", "m2", "m3", "m4", "q", "v", "iv", "rs", "bn", "e", "es", "w", "t", "dya", "u", "o", "std"]
+              "m1", "m2", "m3", "m4", "q", "bi", "ds", "v", "iv", "sd", "e", "es", "w", "t", "dya", "u", "o", "std"]
 
 ADD, SUB, MUL = AluOpType.add, AluOpType.subtract, AluOpType.mult
 X = AxisListType.X
@@ -108,22 +108,25 @@ def rank_program(g, core, T, topo):
     PE.matmul(T.P3[:, 0:17], T.G[:, 2:512:4], T.Wc[:, 17:34], True, True).then_inc(S.m3, 1)
     PE.matmul(T.P4[:, 0:1], T.G[:, 3:512:4], T.Wc[:, 35:36], True, True).then_inc(S.m4, 1)
 
-    q, vv, iv, rs, es, w = (T.sc[:, k:k + 1] for k in range(6))
+    q, bi, vv, iv, sd, es, w = (T.sc[:, k:k + 1] for k in range(7))
     A.wait_ge(S.m1, 1)
     A.activation(T.jc[:], T.P1[:, 0:N], ACT.Square, scale=0.25, accum_out=q).then_inc(S.q, 1)
-    V.wait_ge(S.q, 1)
     V.wait_ge(S.m2, 1)
-    V.tensor_scalar(vv, q, T.P2[:, 0:1], EPS, ADD, ADD).then_inc(S.v, 1)
+    V.tensor_scalar(bi, T.P2[:, 0:1], EPS, None, ADD).then_inc(S.bi, 1)
+    A.wait_ge(S.q, 1)
+    A.wait_ge(S.bi, 1)
+    A.activation(sd, q, ACT.Sqrt, bias=bi).then_inc(S.sd, 1)
+
+    V.wait_ge(S.q, 1)
+    V.tensor_copy(T.dS[:], T.P1[:, 0:N + 1]).then_inc(S.ds, 1)
+    V.wait_ge(S.bi, 1)
+    V.tensor_scalar(vv, q, bi, None, ADD).then_inc(S.v, 1)
+    V.wait_ge(S.ds, 1)
+    V.wait_ge(S.m3, 1)
+    V.tensor_tensor(T.ee[:], T.dS[:, 0:N], T.P3[:, 0:N], MUL).then_inc(S.e, 1)
+    V.tensor_scalar(T.dya[:], T.dys[:], T.P3[:, N:N + 1], None, SUB).then_inc(S.dya, 1)
     V.wait_ge(S.v, 1)
     V.reciprocal(iv, vv).then_inc(S.iv, 1)
-    A.wait_ge(S.iv, 1)
-    A.activation(rs, iv, ACT.Sqrt).then_inc(S.rs, 1)
-
-    V.wait_ge(S.m3, 1)
-    V.tensor_copy(T.bn[:], T.P3[:, 0:17]).then_inc(S.bn, 1)
-    V.wait_ge(S.bn, 1)
-    V.tensor_scalar(T.dya[:], T.dys[:], T.bn[:, 16:17], None, SUB).then_inc(S.dya, 1)
-    V.tensor_tensor(T.ee[:], T.P1[:, 0:N], T.bn[:, 0:N], MUL).then_inc(S.e, 1)
     V.wait_ge(S.e, 1)
     V.tensor_reduce(es, T.ee[:], X, ADD).then_inc(S.es, 1)
     V.wait_ge(S.es, 1)
@@ -131,15 +134,15 @@ def rank_program(g, core, T, topo):
     V.wait_ge(S.iv, 1)
     V.tensor_scalar(w, es, T.P4[:, 0:1], iv, ADD, MUL).then_inc(S.w, 1)
     V.wait_ge(S.w, 1)
-    V.tensor_scalar(T.tP[:, 0:TK], T.xs[:], T.P1[:, 16:17], w, SUB, MUL).then_inc(S.t, 1)
+    V.tensor_scalar(T.tP[:, 0:TK], T.xs[:], T.dS[:, N:N + 1], w, SUB, MUL).then_inc(S.t, 1)
     V.wait_ge(S.t, 1)
     V.wait_ge(S.dya, 1)
     V.tensor_tensor(T.uu[:], T.dya[:], T.tP[:, 0:TK], SUB).then_inc(S.u, 1)
+    V.wait_ge(S.u, 1)
+    V.wait_ge(S.sd, 1)
+    V.tensor_scalar(T.oo[:], T.uu[:], sd, iv, MUL, MUL).then_inc(S.o, 1)
 
-    A.wait_ge(S.rs, 1)
-    A.wait_ge(S.u, 1)
-    A.activation(T.oo[:], T.uu[:], ACT.Copy, scale=rs).then_inc(S.o, 1)
-    A.wait_ge(S.o, 1)
-    A.dma_start(T.dx[:], T.oo[:]).then_inc(S.std, 16)
-    A.wait_ge(S.std, 16)
+    SY.wait_ge(S.o, 1)
+    SY.dma_start(T.dx[:], T.oo[:]).then_inc(S.std, 16)
+    SY.wait_ge(S.std, 16)
     g.wait_ge(S.sent, len(engines))

@@ -12,26 +12,23 @@ SCRATCH = {
     "st": ("sbuf", [128, 4], "float32"),
     "gath": ("dram", [N, 128, 4], "float32"),
     "G": ("sbuf", [N, 512], "float32"),
-    "Wc": ("sbuf", [N, 36], "float32"),
+    "Wc": ("sbuf", [N, 20], "float32"),
     "ja": ("sbuf", [128, TK], "float32"),
     "jb": ("sbuf", [128, TK], "float32"),
     "jc": ("sbuf", [128, N], "float32"),
     "pr": ("sbuf", [128, TK], "float32"),
-    "dS": ("sbuf", [128, N + 1], "float32"),
-    "ee": ("sbuf", [128, N], "float32"),
     "sc": ("sbuf", [128, 8], "float32"),
+    "xm": ("sbuf", [128, TK], "float32"),
     "dya": ("sbuf", [128, TK], "float32"),
     "uu": ("sbuf", [128, TK], "float32"),
     "oo": ("sbuf", [128, TK], "float32"),
-    "yP": ("psum", [128, 512], "float32"),
     "tP": ("psum", [128, 512], "float32"),
     "P1": ("psum", [128, 512], "float32"),
     "P2": ("psum", [128, 512], "float32"),
     "P3": ("psum", [128, 512], "float32"),
-    "P4": ("psum", [128, 512], "float32"),
 }
-SEMAPHORES = ["ldx", "ldy", "cst", "cst2", "s_sx", "s_y", "s_pr", "s_st", "stq", "sent", "arr", "gl",
-              "m1", "m2", "m3", "m4", "q", "bi", "ds", "v", "iv", "sd", "e", "es", "w", "t", "dya", "u", "o", "std"]
+SEMAPHORES = ["ldx", "ldy", "cst", "cst2", "s_sx", "s_pr", "s_st", "stq", "sent", "arr", "gl",
+              "m1", "m2", "m3", "m4", "q", "bi", "v", "iv", "sd", "nsb", "xm", "t", "dya", "u", "o", "std"]
 
 ADD, SUB, MUL = AluOpType.add, AluOpType.subtract, AluOpType.mult
 X = AxisListType.X
@@ -50,21 +47,15 @@ def rank_program(g, core, T, topo):
 
     V.memset(T.Wc[:, 0:16], 1.0 / NT).then_inc(S.cst, 1)
     V.memset(T.Wc[:, 16:17], -1.0 / NT).then_inc(S.cst, 1)
-    V.memset(T.Wc[:, 17:33], 0.0).then_inc(S.cst, 1)
-    V.memset(T.Wc[:, 33:34], 1.0 / NT).then_inc(S.cst, 1)
-    V.memset(T.Wc[:, 34:35], 1.0 / (NT * TK * TK)).then_inc(S.cst, 1)
-    V.memset(T.Wc[:, 35:36], 1.0 / (NT * TK)).then_inc(S.cst, 1)
-    g.wait_ge(S.cst, 6)
+    V.memset(T.Wc[:, 17:18], 1.0 / (NT * TK * TK)).then_inc(S.cst, 1)
+    V.memset(T.Wc[:, 18:19], 1.0 / NT).then_inc(S.cst, 1)
+    g.wait_ge(S.cst, 4)
     g.affine_select(T.Wc[:, 0:16], T.Wc[:, 0:16], [[-1, N]], AluOpType.not_equal, 1.0 / NT - 1.0 / TK, 0, 1).then_inc(S.cst2, 1)
-    g.affine_select(T.Wc[:, 17:33], T.Wc[:, 17:33], [[-1, N]], AluOpType.not_equal, 1.0 / NT, 0, 1).then_inc(S.cst2, 1)
 
     V.wait_ge(S.ldx, 16)
     V.tensor_reduce(T.st[:, 0:1], T.xs[:], X, ADD, negate=True).then_inc(S.s_sx, 1)
-    V.wait_ge(S.s_sx, 1)
-    V.tensor_scalar(T.yP[:, 0:TK], T.xs[:], float(TK), T.st[:, 0:1], MUL, ADD).then_inc(S.s_y, 1)
-    V.wait_ge(S.s_y, 1)
     V.wait_ge(S.ldy, 16)
-    V.tensor_tensor(T.pr[:], T.yP[:, 0:TK], T.dys[:], MUL).then_inc(S.s_pr, 1)
+    V.tensor_tensor(T.pr[:], T.xs[:], T.dys[:], MUL).then_inc(S.s_pr, 1)
     V.wait_ge(S.s_pr, 1)
     V.tensor_reduce(T.st[:, 3:4], T.pr[:], X, ADD).then_inc(S.s_st, 1)
 
@@ -100,15 +91,16 @@ def rank_program(g, core, T, topo):
     SY.wait_ge(S.arr, N - 1)
     SY.dma_start(T.G[:], T.gath[:]).then_inc(S.gl, 16)
 
-    PE.wait_ge(S.cst, 6)
-    PE.wait_ge(S.cst2, 2)
+    PE.wait_ge(S.cst, 4)
+    PE.wait_ge(S.cst2, 1)
     PE.wait_ge(S.gl, 16)
     PE.matmul(T.P1[:, 0:17], T.G[:, 0:512:4], T.Wc[:, 0:17], True, True).then_inc(S.m1, 1)
-    PE.matmul(T.P2[:, 0:1], T.G[:, 1:512:4], T.Wc[:, 34:35], True, True).then_inc(S.m2, 1)
-    PE.matmul(T.P3[:, 0:17], T.G[:, 2:512:4], T.Wc[:, 17:34], True, True).then_inc(S.m3, 1)
-    PE.matmul(T.P4[:, 0:1], T.G[:, 3:512:4], T.Wc[:, 35:36], True, True).then_inc(S.m4, 1)
+    PE.matmul(T.P2[:, 0:1], T.G[:, 1:512:4], T.Wc[:, 17:18], True, True).then_inc(S.m2, 1)
+    PE.matmul(T.P3[:, 0:1], T.G[:, 2:512:4], T.Wc[:, 18:19], True, True).then_inc(S.m3, 1)
+    PE.matmul(T.P3[:, 1:2], T.G[:, 3:512:4], T.Wc[:, 18:19], True, True).then_inc(S.m4, 1)
 
-    q, bi, vv, iv, sd, es, w = (T.sc[:, k:k + 1] for k in range(7))
+    q, bi, vv, iv, sd, nsb = (T.sc[:, k:k + 1] for k in range(6))
+    mu, a, cm = T.P1[:, N:N + 1], T.P3[:, 0:1], T.P3[:, 1:2]
     A.wait_ge(S.m1, 1)
     A.activation(T.jc[:], T.P1[:, 0:N], ACT.Square, scale=0.25, accum_out=q).then_inc(S.q, 1)
     V.wait_ge(S.m2, 1)
@@ -118,26 +110,22 @@ def rank_program(g, core, T, topo):
     A.activation(sd, q, ACT.Sqrt, bias=bi).then_inc(S.sd, 1)
 
     V.wait_ge(S.q, 1)
-    V.tensor_copy(T.dS[:], T.P1[:, 0:N + 1]).then_inc(S.ds, 1)
     V.wait_ge(S.bi, 1)
     V.tensor_scalar(vv, q, bi, None, ADD).then_inc(S.v, 1)
-    V.wait_ge(S.ds, 1)
     V.wait_ge(S.m3, 1)
-    V.tensor_tensor(T.ee[:], T.dS[:, 0:N], T.P3[:, 0:N], MUL).then_inc(S.e, 1)
-    V.tensor_scalar(T.dya[:], T.dys[:], T.P3[:, N:N + 1], None, SUB).then_inc(S.dya, 1)
+    V.wait_ge(S.m4, 1)
+    V.tensor_scalar(nsb, mu, a, cm, MUL, SUB).then_inc(S.nsb, 1)
+    V.tensor_scalar(T.xm[:], T.xs[:], mu, None, SUB).then_inc(S.xm, 1)
+    V.tensor_scalar(T.dya[:], T.dys[:], a, None, SUB).then_inc(S.dya, 1)
     V.wait_ge(S.v, 1)
     V.reciprocal(iv, vv).then_inc(S.iv, 1)
-    V.wait_ge(S.e, 1)
-    V.tensor_reduce(es, T.ee[:], X, ADD).then_inc(S.es, 1)
-    V.wait_ge(S.es, 1)
-    V.wait_ge(S.m4, 1)
     V.wait_ge(S.iv, 1)
-    V.tensor_scalar(w, es, T.P4[:, 0:1], iv, ADD, MUL).then_inc(S.w, 1)
-    V.wait_ge(S.w, 1)
-    V.tensor_scalar(T.tP[:, 0:TK], T.xs[:], T.dS[:, N:N + 1], w, SUB, MUL).then_inc(S.t, 1)
+    V.wait_ge(S.nsb, 1)
+    V.wait_ge(S.xm, 1)
+    V.tensor_scalar(T.tP[:, 0:TK], T.xm[:], nsb, iv, MUL, MUL).then_inc(S.t, 1)
     V.wait_ge(S.t, 1)
     V.wait_ge(S.dya, 1)
-    V.tensor_tensor(T.uu[:], T.dya[:], T.tP[:, 0:TK], SUB).then_inc(S.u, 1)
+    V.tensor_tensor(T.uu[:], T.dya[:], T.tP[:, 0:TK], ADD).then_inc(S.u, 1)
     V.wait_ge(S.u, 1)
     V.wait_ge(S.sd, 1)
     V.tensor_scalar(T.oo[:], T.uu[:], sd, iv, MUL, MUL).then_inc(S.o, 1)

@@ -1,3 +1,5 @@
+import math
+
 from concourse.bass import DstId, RemoteDMATransfer
 from concourse.mybir import AluOpType, AxisListType, ActivationFunctionType
 
@@ -9,9 +11,12 @@ EPS = 0.01
 SCRATCH = {
     "xs": ("sbuf", [128, TK], "float32"),
     "dys": ("sbuf", [128, TK], "float32"),
-    "st": ("sbuf", [128, 4], "float32"),
-    "gath": ("dram", [N, 128, 4], "float32"),
-    "G": ("sbuf", [N, 512], "float32"),
+    "stA": ("sbuf", [128, 2], "float32"),
+    "stB": ("sbuf", [128, 2], "float32"),
+    "gA": ("dram", [N, 128, 2], "float32"),
+    "gB": ("dram", [N, 128, 2], "float32"),
+    "GA": ("sbuf", [N, 256], "float32"),
+    "GB": ("sbuf", [N, 256], "float32"),
     "Wc": ("sbuf", [N, 20], "float32"),
     "ja": ("sbuf", [128, TK], "float32"),
     "jb": ("sbuf", [128, TK], "float32"),
@@ -20,15 +25,19 @@ SCRATCH = {
     "sc": ("sbuf", [128, 8], "float32"),
     "xm": ("sbuf", [128, TK], "float32"),
     "dya": ("sbuf", [128, TK], "float32"),
+    "pp": ("sbuf", [128, TK], "float32"),
     "uu": ("sbuf", [128, TK], "float32"),
     "oo": ("sbuf", [128, TK], "float32"),
     "tP": ("psum", [128, 512], "float32"),
     "P1": ("psum", [128, 512], "float32"),
     "P2": ("psum", [128, 512], "float32"),
+    "P2b": ("psum", [128, 512], "float32"),
     "P3": ("psum", [128, 512], "float32"),
+    "P4": ("psum", [128, 512], "float32"),
 }
-SEMAPHORES = ["ldx", "ldy", "cst", "cst2", "s_sx", "s_pr", "s_st", "stq", "sent", "arr", "gl",
-              "m1", "m2", "m3", "m4", "q", "bi", "v", "iv", "sd", "nsb", "xm", "t", "dya", "u", "o", "std"]
+SEMAPHORES = ["ldx", "ldy", "cst", "cst2", "s_sx", "s_b", "s_pr", "s_m2", "s_c", "qA", "qB", "sent", "arrA", "arrB",
+              "glA", "glB", "m1", "m2", "m2b", "m3", "m4", "q", "v", "iv", "k", "sd", "nsb", "xm", "dya", "p", "t",
+              "u", "o", "std"]
 
 ADD, SUB, MUL = AluOpType.add, AluOpType.subtract, AluOpType.mult
 X = AxisListType.X
@@ -53,21 +62,24 @@ def rank_program(g, core, T, topo):
     g.affine_select(T.Wc[:, 0:16], T.Wc[:, 0:16], [[-1, N]], AluOpType.not_equal, 1.0 / NT - 1.0 / TK, 0, 1).then_inc(S.cst2, 1)
 
     V.wait_ge(S.ldx, 16)
-    V.tensor_reduce(T.st[:, 0:1], T.xs[:], X, ADD, negate=True).then_inc(S.s_sx, 1)
+    V.tensor_reduce(T.stA[:, 0:1], T.xs[:], X, ADD, negate=True).then_inc(S.s_sx, 1)
     V.wait_ge(S.ldy, 16)
     V.tensor_tensor(T.pr[:], T.xs[:], T.dys[:], MUL).then_inc(S.s_pr, 1)
     V.wait_ge(S.s_pr, 1)
-    V.tensor_reduce(T.st[:, 3:4], T.pr[:], X, ADD).then_inc(S.s_st, 1)
+    V.tensor_reduce(T.stB[:, 1:2], T.pr[:], X, ADD).then_inc(S.s_c, 1)
 
     A.wait_ge(S.ldy, 16)
-    A.activation(T.ja[:], T.dys[:], ACT.Copy, accum_out=T.st[:, 2:3]).then_inc(S.s_st, 1)
+    A.activation(T.ja[:], T.dys[:], ACT.Copy, accum_out=T.stA[:, 1:2]).then_inc(S.s_b, 1)
     A.wait_ge(S.ldx, 16)
     A.wait_ge(S.s_sx, 1)
-    A.activation(T.jb[:], T.xs[:], ACT.Square, bias=T.st[:, 0:1], scale=float(TK), accum_out=T.st[:, 1:2]).then_inc(S.s_st, 1)
+    A.activation(T.jb[:], T.xs[:], ACT.Square, bias=T.stA[:, 0:1], scale=float(TK), accum_out=T.stB[:, 0:1]).then_inc(S.s_m2, 1)
 
     SY.wait_ge(S.s_sx, 1)
-    SY.wait_ge(S.s_st, 3)
-    SY.dma_start(T.gath[rank], T.st[:]).then_inc(S.stq, 16)
+    SY.wait_ge(S.s_b, 1)
+    SY.dma_start(T.gA[rank], T.stA[:]).then_inc(S.qA, 16)
+    SY.wait_ge(S.s_m2, 1)
+    SY.wait_ge(S.s_c, 1)
+    SY.dma_start(T.gB[rank], T.stB[:]).then_inc(S.qB, 16)
 
     others = [T.cores[(rank + k) % N] for k in range(1, N)]
     allowed = topo.mask(core, others[0])
@@ -75,62 +87,78 @@ def rank_program(g, core, T, topo):
         allowed &= topo.mask(core, d)
     engines = [e for e in range(16) if (allowed >> e) & 1]
     engines = engines[::max(1, len(engines) // 4)][:4]
-    transfers = []
-    for j, e in enumerate(engines):
-        mine = others[j::len(engines)]
-        ids = []
-        for d in mine:
-            rid, pid = topo.addr(d, core)
-            ids.append(DstId(rid=rid, pnc=pid))
-        transfers.append(RemoteDMATransfer(dst_ids=ids, dma_engine_mask=1 << e, remote_sem=S.arr,
-                                           srcs=[T.gath[rank]], dsts=[T.gath[rank] for _ in mine], alu_op=0))
-    g.wait_ge(S.stq, 16)
-    g.remote_dma_fused(transfers, local_sem=S.sent)
 
-    SY.wait_ge(S.stq, 16)
-    SY.wait_ge(S.arr, N - 1)
-    SY.dma_start(T.G[:], T.gath[:]).then_inc(S.gl, 16)
+    def spread(slot, arrived):
+        transfers = []
+        for j, e in enumerate(engines):
+            mine = others[j::len(engines)]
+            ids = []
+            for d in mine:
+                rid, pid = topo.addr(d, core)
+                ids.append(DstId(rid=rid, pnc=pid))
+            transfers.append(RemoteDMATransfer(dst_ids=ids, dma_engine_mask=1 << e, remote_sem=arrived,
+                                               srcs=[slot], dsts=[slot for _ in mine], alu_op=0))
+        g.remote_dma_fused(transfers, local_sem=S.sent)
+
+    g.wait_ge(S.qA, 16)
+    spread(T.gA[rank], S.arrA)
+    g.wait_ge(S.qB, 16)
+    spread(T.gB[rank], S.arrB)
+
+    SY.wait_ge(S.qA, 16)
+    SY.wait_ge(S.arrA, N - 1)
+    SY.dma_start(T.GA[:], T.gA[:]).then_inc(S.glA, 16)
+    SY.wait_ge(S.qB, 16)
+    SY.wait_ge(S.arrB, N - 1)
+    SY.dma_start(T.GB[:], T.gB[:]).then_inc(S.glB, 16)
 
     PE.wait_ge(S.cst, 4)
     PE.wait_ge(S.cst2, 1)
-    PE.wait_ge(S.gl, 16)
-    PE.matmul(T.P1[:, 0:17], T.G[:, 0:512:4], T.Wc[:, 0:17], True, True).then_inc(S.m1, 1)
-    PE.matmul(T.P2[:, 0:1], T.G[:, 1:512:4], T.Wc[:, 17:18], True, True).then_inc(S.m2, 1)
-    PE.matmul(T.P3[:, 0:1], T.G[:, 2:512:4], T.Wc[:, 18:19], True, True).then_inc(S.m3, 1)
-    PE.matmul(T.P3[:, 1:2], T.G[:, 3:512:4], T.Wc[:, 18:19], True, True).then_inc(S.m4, 1)
+    PE.wait_ge(S.glA, 16)
+    PE.matmul(T.P1[:, 0:17], T.GA[:, 0:256:2], T.Wc[:, 0:17], True, True).then_inc(S.m1, 1)
+    PE.matmul(T.P3[:, 0:1], T.GA[:, 1:256:2], T.Wc[:, 18:19], True, True).then_inc(S.m3, 1)
+    PE.wait_ge(S.glB, 16)
+    PE.matmul(T.P2[:, 0:1], T.GB[:, 0:256:2], T.Wc[:, 17:18], True, True).then_inc(S.m2, 1)
+    PE.matmul(T.P2b[:, 0:1], T.GB[:, 0:256:2], T.Wc[:, 17:18], True, True).then_inc(S.m2b, 1)
+    PE.matmul(T.P4[:, 0:1], T.GB[:, 1:256:2], T.Wc[:, 18:19], True, True).then_inc(S.m4, 1)
 
-    q, bi, vv, iv, sd, nsb = (T.sc[:, k:k + 1] for k in range(6))
-    mu, a, cm = T.P1[:, N:N + 1], T.P3[:, 0:1], T.P3[:, 1:2]
+    q, vv, iv, kk, sd, nsb = (T.sc[:, k:k + 1] for k in range(6))
+    mu, a, cm = T.P1[:, N:N + 1], T.P3[:, 0:1], T.P4[:, 0:1]
+
     A.wait_ge(S.m1, 1)
-    A.activation(T.jc[:], T.P1[:, 0:N], ACT.Square, scale=0.25, accum_out=q).then_inc(S.q, 1)
-    V.wait_ge(S.m2, 1)
-    V.tensor_scalar(bi, T.P2[:, 0:1], EPS, None, ADD).then_inc(S.bi, 1)
-    A.wait_ge(S.q, 1)
-    A.wait_ge(S.bi, 1)
-    A.activation(sd, q, ACT.Sqrt, bias=bi).then_inc(S.sd, 1)
-
+    A.activation(T.jc[:], T.P1[:, 0:N], ACT.Square, bias=math.sqrt(EPS / N), scale=0.25,
+                 accum_out=q).then_inc(S.q, 1)
     V.wait_ge(S.q, 1)
-    V.wait_ge(S.bi, 1)
-    V.tensor_scalar(vv, q, bi, None, ADD).then_inc(S.v, 1)
+    V.tensor_scalar(T.xm[:], T.xs[:], mu, None, SUB).then_inc(S.xm, 1)
     V.wait_ge(S.m3, 1)
+    V.tensor_scalar(T.dya[:], T.dys[:], a, None, SUB).then_inc(S.dya, 1)
+
+    A.wait_ge(S.q, 1)
+    A.wait_ge(S.m2, 1)
+    A.activation(sd, T.P2[:, 0:1], ACT.Sqrt, bias=q).then_inc(S.sd, 1)
+
+    V.wait_ge(S.m2b, 1)
+    V.tensor_scalar(vv, T.P2b[:, 0:1], q, None, ADD).then_inc(S.v, 1)
     V.wait_ge(S.m4, 1)
     V.tensor_scalar(nsb, mu, a, cm, MUL, SUB).then_inc(S.nsb, 1)
-    V.tensor_scalar(T.xm[:], T.xs[:], mu, None, SUB).then_inc(S.xm, 1)
-    V.tensor_scalar(T.dya[:], T.dys[:], a, None, SUB).then_inc(S.dya, 1)
     V.wait_ge(S.v, 1)
     V.reciprocal(iv, vv).then_inc(S.iv, 1)
-    V.wait_ge(S.iv, 1)
+    V.wait_ge(S.dya, 1)
+    V.tensor_scalar(T.pp[:], T.dya[:], vv, None, MUL).then_inc(S.p, 1)
     V.wait_ge(S.nsb, 1)
     V.wait_ge(S.xm, 1)
-    V.tensor_scalar(T.tP[:, 0:TK], T.xm[:], nsb, iv, MUL, MUL).then_inc(S.t, 1)
+    V.tensor_scalar(T.tP[:, 0:TK], T.xm[:], nsb, None, MUL).then_inc(S.t, 1)
+    V.wait_ge(S.iv, 1)
+    V.tensor_scalar(kk, iv, iv, None, MUL).then_inc(S.k, 1)
+    V.wait_ge(S.p, 1)
     V.wait_ge(S.t, 1)
-    V.wait_ge(S.dya, 1)
-    V.tensor_tensor(T.uu[:], T.dya[:], T.tP[:, 0:TK], ADD).then_inc(S.u, 1)
+    V.tensor_tensor(T.uu[:], T.pp[:], T.tP[:, 0:TK], ADD).then_inc(S.u, 1)
     V.wait_ge(S.u, 1)
+    V.wait_ge(S.k, 1)
     V.wait_ge(S.sd, 1)
-    V.tensor_scalar(T.oo[:], T.uu[:], sd, iv, MUL, MUL).then_inc(S.o, 1)
+    V.tensor_scalar(T.oo[:], T.uu[:], sd, kk, MUL, MUL).then_inc(S.o, 1)
 
     SY.wait_ge(S.o, 1)
     SY.dma_start(T.dx[:], T.oo[:]).then_inc(S.std, 16)
     SY.wait_ge(S.std, 16)
-    g.wait_ge(S.sent, len(engines))
+    g.wait_ge(S.sent, 2 * len(engines))

@@ -1,5 +1,3 @@
-import math
-
 from concourse.bass import DstId, RemoteDMATransfer
 from concourse.mybir import AluOpType, AxisListType, ActivationFunctionType
 
@@ -23,21 +21,17 @@ SCRATCH = {
     "jc": ("sbuf", [128, N], "float32"),
     "pr": ("sbuf", [128, TK], "float32"),
     "sc": ("sbuf", [128, 8], "float32"),
-    "xm": ("sbuf", [128, TK], "float32"),
-    "dya": ("sbuf", [128, TK], "float32"),
     "pp": ("sbuf", [128, TK], "float32"),
     "uu": ("sbuf", [128, TK], "float32"),
     "oo": ("sbuf", [128, TK], "float32"),
     "tP": ("psum", [128, 512], "float32"),
     "P1": ("psum", [128, 512], "float32"),
+    "Pm": ("psum", [128, 512], "float32"),
     "P2": ("psum", [128, 512], "float32"),
-    "P2b": ("psum", [128, 512], "float32"),
-    "P3": ("psum", [128, 512], "float32"),
     "P4": ("psum", [128, 512], "float32"),
 }
-SEMAPHORES = ["ldx", "ldy", "cst", "cst2", "s_sx", "s_b", "s_pr", "s_m2", "s_c", "qA", "qB", "sent", "arrA", "arrB",
-              "glA", "glB", "m1", "m2", "m2b", "m3", "m4", "q", "v", "iv", "k", "sd", "nsb", "xm", "dya", "p", "t",
-              "u", "o", "std"]
+SEMAPHORES = ["ldx", "ldy", "cst", "cst2", "cstb", "s_sx", "s_b", "s_pr", "s_m2", "s_c", "qA", "qB", "sent", "arrA", "arrB",
+              "glA", "glB", "m1", "mm", "m2", "m4", "b", "q", "v", "v2", "k", "sd", "nsb", "p", "t", "u", "o", "std"]
 
 ADD, SUB, MUL = AluOpType.add, AluOpType.subtract, AluOpType.mult
 X = AxisListType.X
@@ -50,6 +44,7 @@ def rank_program(g, core, T, topo):
         return
     S = T.sem
     V, A, PE, SY = g.vector, g.scalar, g.tensor, g.sync
+    q, vv, v2, kk, sd, nsb, ec, bc = (T.sc[:, k:k + 1] for k in range(8))
 
     SY.dma_start(T.xs[:], T.x[:]).then_inc(S.ldx, 16)
     A.dma_start(T.dys[:], T.dy[:]).then_inc(S.ldy, 16)
@@ -58,6 +53,7 @@ def rank_program(g, core, T, topo):
     V.memset(T.Wc[:, 16:17], -1.0 / NT).then_inc(S.cst, 1)
     V.memset(T.Wc[:, 17:18], 1.0 / (NT * TK * TK)).then_inc(S.cst, 1)
     V.memset(T.Wc[:, 18:19], 1.0 / NT).then_inc(S.cst, 1)
+    V.memset(ec, EPS / N).then_inc(S.cstb, 1)
     g.wait_ge(S.cst, 4)
     g.affine_select(T.Wc[:, 0:16], T.Wc[:, 0:16], [[-1, N]], AluOpType.not_equal, 1.0 / NT - 1.0 / TK, 0, 1).then_inc(S.cst2, 1)
 
@@ -73,6 +69,8 @@ def rank_program(g, core, T, topo):
     A.wait_ge(S.ldx, 16)
     A.wait_ge(S.s_sx, 1)
     A.activation(T.jb[:], T.xs[:], ACT.Square, bias=T.stA[:, 0:1], scale=float(TK), accum_out=T.stB[:, 0:1]).then_inc(S.s_m2, 1)
+    A.wait_ge(S.cstb, 1)
+    A.activation(bc, ec, ACT.Sqrt).then_inc(S.b, 1)
 
     SY.wait_ge(S.s_sx, 1)
     SY.wait_ge(S.s_b, 1)
@@ -115,41 +113,33 @@ def rank_program(g, core, T, topo):
     PE.wait_ge(S.cst, 4)
     PE.wait_ge(S.cst2, 1)
     PE.wait_ge(S.glA, 16)
-    PE.matmul(T.P1[:, 0:17], T.GA[:, 0:256:2], T.Wc[:, 0:17], True, True).then_inc(S.m1, 1)
-    PE.matmul(T.P3[:, 0:1], T.GA[:, 1:256:2], T.Wc[:, 18:19], True, True).then_inc(S.m3, 1)
+    PE.matmul(T.P1[:, 0:N], T.GA[:, 0:256:2], T.Wc[:, 0:N], True, True).then_inc(S.m1, 1)
+    PE.matmul(T.Pm[:, 0:1], T.GA[:, 0:256:2], T.Wc[:, 16:17], True, True).then_inc(S.mm, 1)
+    PE.matmul(T.Pm[:, 1:2], T.GA[:, 1:256:2], T.Wc[:, 18:19], True, True).then_inc(S.mm, 1)
     PE.wait_ge(S.glB, 16)
-    PE.matmul(T.P2[:, 0:1], T.GB[:, 0:256:2], T.Wc[:, 17:18], True, True).then_inc(S.m2, 1)
-    PE.matmul(T.P2b[:, 0:1], T.GB[:, 0:256:2], T.Wc[:, 17:18], True, True).then_inc(S.m2b, 1)
     PE.matmul(T.P4[:, 0:1], T.GB[:, 1:256:2], T.Wc[:, 18:19], True, True).then_inc(S.m4, 1)
+    PE.matmul(T.P2[:, 0:1], T.GB[:, 0:256:2], T.Wc[:, 17:18], True, True).then_inc(S.m2, 1)
 
-    q, vv, iv, kk, sd, nsb = (T.sc[:, k:k + 1] for k in range(6))
-    mu, a, cm = T.P1[:, N:N + 1], T.P3[:, 0:1], T.P4[:, 0:1]
+    mu, a, cm, m2 = T.Pm[:, 0:1], T.Pm[:, 1:2], T.P4[:, 0:1], T.P2[:, 0:1]
 
     A.wait_ge(S.m1, 1)
-    A.activation(T.jc[:], T.P1[:, 0:N], ACT.Square, bias=math.sqrt(EPS / N), scale=0.25,
-                 accum_out=q).then_inc(S.q, 1)
-    V.wait_ge(S.q, 1)
-    V.tensor_scalar(T.xm[:], T.xs[:], mu, None, SUB).then_inc(S.xm, 1)
-    V.wait_ge(S.m3, 1)
-    V.tensor_scalar(T.dya[:], T.dys[:], a, None, SUB).then_inc(S.dya, 1)
-
+    A.wait_ge(S.b, 1)
+    A.activation(T.jc[:], T.P1[:, 0:N], ACT.Square, bias=bc, scale=0.25, accum_out=q).then_inc(S.q, 1)
     A.wait_ge(S.q, 1)
     A.wait_ge(S.m2, 1)
-    A.activation(sd, T.P2[:, 0:1], ACT.Sqrt, bias=q).then_inc(S.sd, 1)
+    A.activation(vv, m2, ACT.Identity, bias=q).then_inc(S.v, 1)
+    A.activation(v2, m2, ACT.Square, bias=q).then_inc(S.v2, 1)
+    A.activation(sd, m2, ACT.Sqrt, bias=q).then_inc(S.sd, 1)
 
-    V.wait_ge(S.m2b, 1)
-    V.tensor_scalar(vv, T.P2b[:, 0:1], q, None, ADD).then_inc(S.v, 1)
+    V.wait_ge(S.mm, 2)
     V.wait_ge(S.m4, 1)
     V.tensor_scalar(nsb, mu, a, cm, MUL, SUB).then_inc(S.nsb, 1)
-    V.wait_ge(S.v, 1)
-    V.reciprocal(iv, vv).then_inc(S.iv, 1)
-    V.wait_ge(S.dya, 1)
-    V.tensor_scalar(T.pp[:], T.dya[:], vv, None, MUL).then_inc(S.p, 1)
     V.wait_ge(S.nsb, 1)
-    V.wait_ge(S.xm, 1)
-    V.tensor_scalar(T.tP[:, 0:TK], T.xm[:], nsb, None, MUL).then_inc(S.t, 1)
-    V.wait_ge(S.iv, 1)
-    V.tensor_scalar(kk, iv, iv, None, MUL).then_inc(S.k, 1)
+    V.tensor_scalar(T.tP[:, 0:TK], T.xs[:], mu, nsb, SUB, MUL).then_inc(S.t, 1)
+    V.wait_ge(S.v, 1)
+    V.tensor_scalar(T.pp[:], T.dys[:], a, vv, SUB, MUL).then_inc(S.p, 1)
+    V.wait_ge(S.v2, 1)
+    V.reciprocal(kk, v2).then_inc(S.k, 1)
     V.wait_ge(S.p, 1)
     V.wait_ge(S.t, 1)
     V.tensor_tensor(T.uu[:], T.pp[:], T.tP[:, 0:TK], ADD).then_inc(S.u, 1)

@@ -83,13 +83,13 @@ def rank_program(g, core, T, topo):
     allowed = topo.mask(core, others[0])
     for d in others:
         allowed &= topo.mask(core, d)
-    engines = [e for e in range(16) if (allowed >> e) & 1]
-    engines = engines[::max(1, len(engines) // 4)][:4]
+    every = [e for e in range(16) if (allowed >> e) & 1]
+    engines = every[::max(1, len(every) // 4)][:4]
 
-    def spread(slot, arrived):
+    def spread(slot, arrived, dests):
         transfers = []
         for j, e in enumerate(engines):
-            mine = others[j::len(engines)]
+            mine = dests[j::len(engines)]
             ids = []
             for d in mine:
                 rid, pid = topo.addr(d, core)
@@ -98,13 +98,17 @@ def rank_program(g, core, T, topo):
                                                srcs=[slot], dsts=[slot for _ in mine], alu_op=0))
         g.remote_dma_fused(transfers, local_sem=S.sent)
 
+    g.wait_ge(S.s_sx, 1)
+    g.wait_ge(S.s_b, 1)
+    rid, pid = topo.addr(others[0], core)
+    g.remote_dma(T.gA[rank], T.stA[:], S.arrA, S.sent, pid, rid, allowed)
     g.wait_ge(S.qA, 16)
-    spread(T.gA[rank], S.arrA)
+    spread(T.gA[rank], S.arrA, others[1:])
     g.wait_ge(S.qB, 16)
-    spread(T.gB[rank], S.arrB)
+    spread(T.gB[rank], S.arrB, others)
 
     SY.wait_ge(S.qA, 16)
-    SY.wait_ge(S.arrA, N - 1)
+    SY.wait_ge(S.arrA, len(every) + N - 2)
     SY.dma_start(T.GA[:], T.gA[:]).then_inc(S.glA, 16)
     SY.wait_ge(S.qB, 16)
     SY.wait_ge(S.arrB, N - 1)
@@ -151,4 +155,4 @@ def rank_program(g, core, T, topo):
     SY.wait_ge(S.o, 1)
     SY.dma_start(T.dx[:], T.oo[:]).then_inc(S.std, 16)
     SY.wait_ge(S.std, 16)
-    g.wait_ge(S.sent, 2 * len(engines))
+    g.wait_ge(S.sent, len(every) + 2 * len(engines))

from concourse.bass import DstId, RemoteDMATransfer
from concourse.mybir import AluOpType, AxisListType, ActivationFunctionType

N = 16
TK = 128
NT = N * TK
EPS = 0.01

SCRATCH = {
    "xs": ("sbuf", [128, TK], "float32"),
    "dys": ("sbuf", [128, TK], "float32"),
    "stA": ("sbuf", [128, 2], "float32"),
    "stB": ("sbuf", [128, 2], "float32"),
    "gA": ("dram", [N, 128, 2], "float32"),
    "gB": ("dram", [N, 128, 2], "float32"),
    "GA": ("sbuf", [N, 256], "float32"),
    "GB": ("sbuf", [N, 256], "float32"),
    "Wc": ("sbuf", [N, 20], "float32"),
    "ja": ("sbuf", [128, TK], "float32"),
    "jb": ("sbuf", [128, TK], "float32"),
    "jc": ("sbuf", [128, N], "float32"),
    "pr": ("sbuf", [128, TK], "float32"),
    "sc": ("sbuf", [128, 8], "float32"),
    "pp": ("sbuf", [128, TK], "float32"),
    "uu": ("sbuf", [128, TK], "float32"),
    "oo": ("sbuf", [128, TK], "float32"),
    "tP": ("psum", [128, 512], "float32"),
    "P1": ("psum", [128, 512], "float32"),
    "Pm": ("psum", [128, 512], "float32"),
    "P2": ("psum", [128, 512], "float32"),
    "P4": ("psum", [128, 512], "float32"),
}
SEMAPHORES = ["ldx", "ldy", "cst", "cst2", "cstb", "s_sx", "s_b", "s_pr", "s_m2", "s_c", "qA", "qB", "sent", "arrA", "arrB",
              "glA", "glB", "m1", "mm", "m2", "m4", "b", "q", "v", "v2", "k", "sd", "nsb", "p", "t", "u", "o", "std"]

ADD, SUB, MUL = AluOpType.add, AluOpType.subtract, AluOpType.mult
X = AxisListType.X
ACT = ActivationFunctionType


def rank_program(g, core, T, topo):
    rank = T.rank_of(core)
    if rank is None:
        return
    S = T.sem
    V, A, PE, SY = g.vector, g.scalar, g.tensor, g.sync
    q, vv, v2, kk, sd, nsb, ec, bc = (T.sc[:, k:k + 1] for k in range(8))

    SY.dma_start(T.xs[:], T.x[:]).then_inc(S.ldx, 16)
    A.dma_start(T.dys[:], T.dy[:]).then_inc(S.ldy, 16)

    V.memset(T.Wc[:, 0:16], 1.0 / NT).then_inc(S.cst, 1)
    V.memset(T.Wc[:, 16:17], -1.0 / NT).then_inc(S.cst, 1)
    V.memset(T.Wc[:, 17:18], 1.0 / (NT * TK * TK)).then_inc(S.cst, 1)
    V.memset(T.Wc[:, 18:19], 1.0 / NT).then_inc(S.cst, 1)
    V.memset(ec, EPS / N).then_inc(S.cstb, 1)
    g.wait_ge(S.cst, 4)
    g.affine_select(T.Wc[:, 0:16], T.Wc[:, 0:16], [[-1, N]], AluOpType.not_equal, 1.0 / NT - 1.0 / TK, 0, 1).then_inc(S.cst2, 1)

    V.wait_ge(S.ldx, 16)
    V.tensor_reduce(T.stA[:, 0:1], T.xs[:], X, ADD, negate=True).then_inc(S.s_sx, 1)
    V.wait_ge(S.ldy, 16)
    V.tensor_tensor(T.pr[:], T.xs[:], T.dys[:], MUL).then_inc(S.s_pr, 1)
    V.wait_ge(S.s_pr, 1)
    V.tensor_reduce(T.stB[:, 1:2], T.pr[:], X, ADD).then_inc(S.s_c, 1)

    A.wait_ge(S.ldy, 16)
    A.activation(T.ja[:], T.dys[:], ACT.Copy, accum_out=T.stA[:, 1:2]).then_inc(S.s_b, 1)
    A.wait_ge(S.ldx, 16)
    A.wait_ge(S.s_sx, 1)
    A.activation(T.jb[:], T.xs[:], ACT.Square, bias=T.stA[:, 0:1], scale=float(TK), accum_out=T.stB[:, 0:1]).then_inc(S.s_m2, 1)
    A.wait_ge(S.cstb, 1)
    A.activation(bc, ec, ACT.Sqrt).then_inc(S.b, 1)

    SY.wait_ge(S.s_sx, 1)
    SY.wait_ge(S.s_b, 1)
    SY.dma_start(T.gA[rank], T.stA[:]).then_inc(S.qA, 16)
    SY.wait_ge(S.s_m2, 1)
    SY.wait_ge(S.s_c, 1)
    SY.dma_start(T.gB[rank], T.stB[:]).then_inc(S.qB, 16)

    others = [T.cores[(rank + k) % N] for k in range(1, N)]
    allowed = topo.mask(core, others[0])
    for d in others:
        allowed &= topo.mask(core, d)
    every = [e for e in range(16) if (allowed >> e) & 1]
    engines = every[::max(1, len(every) // 4)][:4]

    def spread(slot, arrived, dests):
        transfers = []
        for j, e in enumerate(engines):
            mine = dests[j::len(engines)]
            ids = []
            for d in mine:
                rid, pid = topo.addr(d, core)
                ids.append(DstId(rid=rid, pnc=pid))
            transfers.append(RemoteDMATransfer(dst_ids=ids, dma_engine_mask=1 << e, remote_sem=arrived,
                                               srcs=[slot], dsts=[slot for _ in mine], alu_op=0))
        g.remote_dma_fused(transfers, local_sem=S.sent)

    g.wait_ge(S.s_sx, 1)
    g.wait_ge(S.s_b, 1)
    rid, pid = topo.addr(others[0], core)
    g.remote_dma(T.gA[rank], T.stA[:], S.arrA, S.sent, pid, rid, allowed)
    g.wait_ge(S.qA, 16)
    spread(T.gA[rank], S.arrA, others[1:])
    g.wait_ge(S.qB, 16)
    spread(T.gB[rank], S.arrB, others)

    SY.wait_ge(S.qA, 16)
    SY.wait_ge(S.arrA, len(every) + N - 2)
    SY.dma_start(T.GA[:], T.gA[:]).then_inc(S.glA, 16)
    SY.wait_ge(S.qB, 16)
    SY.wait_ge(S.arrB, N - 1)
    SY.dma_start(T.GB[:], T.gB[:]).then_inc(S.glB, 16)

    PE.wait_ge(S.cst, 4)
    PE.wait_ge(S.cst2, 1)
    PE.wait_ge(S.glA, 16)
    PE.matmul(T.P1[:, 0:N], T.GA[:, 0:256:2], T.Wc[:, 0:N], True, True).then_inc(S.m1, 1)
    PE.matmul(T.Pm[:, 0:1], T.GA[:, 0:256:2], T.Wc[:, 16:17], True, True).then_inc(S.mm, 1)
    PE.matmul(T.Pm[:, 1:2], T.GA[:, 1:256:2], T.Wc[:, 18:19], True, True).then_inc(S.mm, 1)
    PE.wait_ge(S.glB, 16)
    PE.matmul(T.P4[:, 0:1], T.GB[:, 1:256:2], T.Wc[:, 18:19], True, True).then_inc(S.m4, 1)
    PE.matmul(T.P2[:, 0:1], T.GB[:, 0:256:2], T.Wc[:, 17:18], True, True).then_inc(S.m2, 1)

    mu, a, cm, m2 = T.Pm[:, 0:1], T.Pm[:, 1:2], T.P4[:, 0:1], T.P2[:, 0:1]

    A.wait_ge(S.m1, 1)
    A.wait_ge(S.b, 1)
    A.activation(T.jc[:], T.P1[:, 0:N], ACT.Square, bias=bc, scale=0.25, accum_out=q).then_inc(S.q, 1)
    A.wait_ge(S.q, 1)
    A.wait_ge(S.m2, 1)
    A.activation(vv, m2, ACT.Identity, bias=q).then_inc(S.v, 1)
    A.activation(v2, m2, ACT.Square, bias=q).then_inc(S.v2, 1)
    A.activation(sd, m2, ACT.Sqrt, bias=q).then_inc(S.sd, 1)

    V.wait_ge(S.mm, 2)
    V.wait_ge(S.m4, 1)
    V.tensor_scalar(nsb, mu, a, cm, MUL, SUB).then_inc(S.nsb, 1)
    V.wait_ge(S.nsb, 1)
    V.tensor_scalar(T.tP[:, 0:TK], T.xs[:], mu, nsb, SUB, MUL).then_inc(S.t, 1)
    V.wait_ge(S.v, 1)
    V.tensor_scalar(T.pp[:], T.dys[:], a, vv, SUB, MUL).then_inc(S.p, 1)
    V.wait_ge(S.v2, 1)
    V.reciprocal(kk, v2).then_inc(S.k, 1)
    V.wait_ge(S.p, 1)
    V.wait_ge(S.t, 1)
    V.tensor_tensor(T.uu[:], T.pp[:], T.tP[:, 0:TK], ADD).then_inc(S.u, 1)
    V.wait_ge(S.u, 1)
    V.wait_ge(S.k, 1)
    V.wait_ge(S.sd, 1)
    V.tensor_scalar(T.oo[:], T.uu[:], sd, kk, MUL, MUL).then_inc(S.o, 1)

    SY.wait_ge(S.o, 1)
    SY.dma_start(T.dx[:], T.oo[:]).then_inc(S.std, 16)
    SY.wait_ge(S.std, 16)
    g.wait_ge(S.sent, len(every) + 2 * len(engines))
